import numpy as np
import ml_dtypes


def mxq(x, axis, fmt="e4m3"):
    dtype, down = {"e4m3": (ml_dtypes.float8_e4m3fn, 7), "e5m2": (ml_dtypes.float8_e5m2, 14)}[fmt]
    v = np.moveaxis(np.asarray(x, np.float32).astype(ml_dtypes.bfloat16).astype(np.float64), axis, -1)
    blocks = v.reshape(v.shape[:-1] + (-1, 32))
    amax = np.abs(blocks).max(-1, keepdims=True)
    byte = np.maximum(np.where(amax > 0, np.frexp(amax)[1] - 1 + 127, 0) - down, 1)
    scale = np.exp2(byte - 127.0)
    codes = (blocks / scale).astype(np.float32).astype(dtype).astype(np.float64)
    return np.moveaxis((codes * scale).reshape(v.shape), -1, axis)


WIDE = False


def mx_kscale(k):
    if not WIDE:
        return np.ones(k)
    levels = np.array([30, -30])
    if k % 512:
        return np.exp2(np.random.permutation(np.resize(levels, k // 32))).repeat(32)
    a = np.empty((k // 512, 16))
    for p in range(k // 512):
        a[p, :8] = np.random.permutation(np.resize(levels, 8))
        for g in range(8):
            far = levels[np.abs(levels - a[p, g]) >= 10]
            a[p, g + 8] = far[np.random.randint(len(far))]
    return np.exp2(a.ravel()).repeat(32)


def f64(x):
    return np.asarray(x).astype(np.float64)


def striped(idx):
    return np.tile(np.asarray(idx).reshape(-1, 16).T, (8, 1)).astype(np.uint16)


def unstriped(offs):
    return offs[:16].T.reshape(-1).astype(np.int64)


E2M1 = np.array([0.0, 0.5, 1.0, 1.5, 2.0, 3.0, 4.0, 6.0, -0.0, -0.5, -1.0, -1.5, -2.0, -3.0, -4.0, -6.0])


def pack_weight(w, fmt):
    k, n = w.shape
    w = f64(np.asarray(w, np.float32).astype(ml_dtypes.bfloat16)).reshape(k // 32, 32, n)
    amax = np.abs(w).max(1)
    if fmt in ("e4m3", "e5m2"):
        byte = np.frexp(amax)[1] - 1 + 127 - (7 if fmt == "e4m3" else 14)
    else:
        mant, ex = np.frexp(amax / 6.0)
        byte = np.where(mant > 0.5, ex, ex - 1) + 127
    byte = np.clip(np.where(amax > 0, byte, 1), 1, 254)
    scaled = (w * np.exp2(127.0 - byte)[:, None, :]).reshape(k, n).astype(np.float32)
    by_word = np.ascontiguousarray(scaled.reshape(k // 512, 128, 4, n).transpose(0, 1, 3, 2))
    if fmt in ("e4m3", "e5m2"):
        words = by_word.astype(ml_dtypes.float8_e4m3fn if fmt == "e4m3" else ml_dtypes.float8_e5m2).view(np.uint8)
    else:
        c = by_word.astype(ml_dtypes.float4_e2m1fn).view(np.uint8) & 0xF
        words = (c[..., 0::2] | (c[..., 1::2] << 4)).reshape(k // 512, 128, 2 * n)
    return np.ascontiguousarray(words), np.ascontiguousarray(byte.astype(np.uint8).reshape(k // 512, 16, n))


def unpack_weight(words, scales, fmt):
    g, _, n = scales.shape
    words = np.ascontiguousarray(words).reshape(g, 128, n, -1)
    if fmt in ("e4m3", "e5m2"):
        vals = words.view(ml_dtypes.float8_e4m3fn if fmt == "e4m3" else ml_dtypes.float8_e5m2).astype(np.float64)
    else:
        nib = np.empty((g, 128, n, 4), np.uint8)
        nib[..., 0::2] = words & 0xF
        nib[..., 1::2] = words >> 4
        vals = E2M1[nib]
    vals = vals * np.repeat(np.exp2(scales.astype(np.float64) - 127.0), 8, axis=1)[..., None]
    return vals.transpose(0, 1, 3, 2).reshape(g * 512, n)


def e4m3fn_bytes(y):
    return np.clip(np.asarray(y, np.float64), -448.0, 448.0).astype(np.float32).astype(ml_dtypes.float8_e4m3fn).view(np.uint8)


def e4m3fn_values(b):
    return np.asarray(b, np.uint8).view(ml_dtypes.float8_e4m3fn).astype(np.float64)


K, T, J, R, V, D, N = 512, 1024, 256, 512, 1024, 1024, 256


def setup_inputs():
    n = np.random.standard_normal
    idx = np.random.permutation(T)[:J]
    idx2 = np.random.permutation(V)[:J]
    idx3 = np.random.permutation(D)[:J]
    fk = mx_kscale(K)
    fr = mx_kscale(R)
    xtp = pack_weight(n((K, T)) / fk[:, None], "e2m1")
    wp = pack_weight(n((K, R)) * 1 / np.sqrt(K) * fk[:, None], "e4m3")
    w2p = pack_weight(n((K, R)) * 1 / np.sqrt(K) * fk[:, None], "e5m2")
    wbp = pack_weight(n((R, N)) * 1 / np.sqrt(R) / fr[:, None], "e2m1")
    return {
        "xt_words": xtp[0],
        "xt_scales": xtp[1],
        "w_words": wp[0],
        "w_scales": wp[1],
        "w2_words": w2p[0],
        "w2_scales": w2p[1],
        "ca": e4m3fn_bytes(60.0 * n((R, V))),
        "cb": e4m3fn_bytes(60.0 * n((R, D))),
        "sa": (np.random.uniform(0.004, 0.012, (R, 1)) * fr[:, None]).astype(np.float32),
        "sb": (np.random.uniform(0.004, 0.012, (R, 1)) * fr[:, None]).astype(np.float32),
        "wb_words": wbp[0],
        "wb_scales": wbp[1],
        "offs": striped(idx),
        "offs2": striped(idx2),
        "offs3": striped(idx3),
    }


def reference(xt_words, xt_scales, w_words, w_scales, w2_words, w2_scales, ca, cb, sa, sb, wb_words, wb_scales, offs, offs2, offs3):
    idx = unstriped(offs)
    idx2 = unstriped(offs2)
    idx3 = unstriped(offs3)
    xtu = unpack_weight(xt_words, xt_scales, "e2m1")
    wu = unpack_weight(w_words, w_scales, "e4m3")
    w2u = unpack_weight(w2_words, w2_scales, "e5m2")
    wbu = unpack_weight(wb_words, wb_scales, "e2m1")
    xtidxg = xtu[:, idx]
    a = wu.T @ xtidxg
    b = w2u.T @ xtidxg
    ga = e4m3fn_values(ca)[:, idx2] * f64(sa)
    gb = e4m3fn_values(cb)[:, idx3] * f64(sb)
    hid = np.maximum(a * ga, b * gb)
    hidq = mxq(hid, 0, "e5m2")
    p = wbu.T @ hidq
    return p

@@ -1,0 +1,165 @@
+from contextlib import ExitStack
+
+import concourse.mybir as mybir
+
+K, T, J, R, V, D, N = 512, 1024, 256, 512, 1024, 1024, 256
+FLOPS = 2 * (2 * K * R * J) + 2 * R * N * J
+
+F32 = mybir.dt.float32
+BF16 = mybir.dt.bfloat16
+I32 = mybir.dt.int32
+U32 = mybir.dt.uint32
+U16 = mybir.dt.uint16
+U8 = mybir.dt.uint8
+FP8 = mybir.dt.float8_e4m3fn
+E4M3X4 = mybir.dt.float8_e4m3fn_x4
+E5M2X4 = mybir.dt.float8_e5m2_x4
+E2M1X4 = mybir.dt.float4_e2m1fn_x4
+MULT = mybir.AluOpType.mult
+MAX = mybir.AluOpType.max
+COPY = mybir.ActivationFunctionType.Copy
+
+P = 128
+PACK = 4
+HALF = J // 2
+
+
+def load_scales(queue, plane, scales):
+    for r in range(4):
+        queue.dma_start(out=plane[r:P:32, :].bitcast(I32), in_=scales[0, r:16:4, :].bitcast(I32))
+
+
+def tile_list_twostores_kernel(
+    tc, xt_words, xt_scales, w_words, w_scales, w2_words, w2_scales, ca, cb, sa, sb,
+    wb_words, wb_scales, offs, offs2, offs3, out,
+):
+    nc = tc.nc
+    with ExitStack() as ctx:
+        keep = ctx.enter_context(tc.tile_pool(name="keep", bufs=1))
+        psum = ctx.enter_context(tc.psum_pool(name="psum", bufs=8))
+
+        list_x = keep.tile([P, J // 16], U16, name="list_x")
+        list_a = keep.tile([P, J // 16], U16, name="list_a")
+        list_b = keep.tile([P, J // 16], U16, name="list_b")
+        x_words = keep.tile([P, T], U16, name="x_words", align_bytes=64)
+        x_plane = keep.tile([P, T], U8, name="x_plane", align_bytes=64)
+        store_a = [keep.tile([P, V], U8, name="store_a%d" % t, align_bytes=64) for t in range(PACK)]
+        store_b = [keep.tile([P, D], U8, name="store_b%d" % t, align_bytes=64) for t in range(PACK)]
+        w_raw = [keep.tile([P, R], U32, name="w_raw%d" % s, align_bytes=64) for s in range(2)]
+        w_plane_raw = [keep.tile([P, R], U8, name="w_plane_raw%d" % s, align_bytes=64) for s in range(2)]
+        w_dealt = [keep.tile([P, R], U32, name="w_dealt%d" % s, align_bytes=64) for s in range(2)]
+        w_plane = [keep.tile([P, R], U8, name="w_plane%d" % s, align_bytes=64) for s in range(2)]
+        steps = [keep.tile([P, PACK], F32, name="steps%d" % s) for s in range(2)]
+        wb_sb = keep.tile([P, 2 * N], U8, name="wb_sb", align_bytes=64)
+        wb_plane = keep.tile([P, N], U8, name="wb_plane", align_bytes=64)
+        xg_words = keep.tile([P, J], U16, name="xg_words", align_bytes=64)
+        xg_plane = keep.tile([P, J], U8, name="xg_plane", align_bytes=64)
+        codes = [keep.tile([P, PACK, J], U8, name="codes%d" % s, align_bytes=64) for s in range(2)]
+        scaled = [keep.tile([P, PACK, J], F32, name="scaled%d" % s, align_bytes=64) for s in range(2)]
+        gated = [keep.tile([P, PACK, J], F32, name="gated%d" % s, align_bytes=64) for s in range(2)]
+
+        ca_rows = ca.rearrange("(p t) v -> t p v", t=PACK)
+        cb_rows = cb.rearrange("(p t) v -> t p v", t=PACK)
+        words_of = [w.rearrange("a p c r -> p (a c r)").bitcast(I32) for w in (w_words, w2_words)]
+
+        for plane in (x_plane, w_plane_raw[0], w_plane_raw[1], wb_plane):
+            nc.vector.memset(plane[:].bitcast(I32), 0)
+
+        nc.gpsimd.dma_start(out=steps[0][:], in_=sa.rearrange("(p t) o -> p (t o)", t=PACK))
+        nc.gpsimd.dma_start(out=steps[1][:], in_=sb.rearrange("(p t) o -> p (t o)", t=PACK))
+        load_scales(nc.gpsimd, w_plane_raw[1], w2_scales)
+
+        nc.sync.dma_start(out=store_a[0][:], in_=ca_rows[0])
+        nc.sync.dma_start(list_a[:], offs2)
+        nc.sync.dma_start(list_x[:], offs)
+        nc.sync.dma_start(out=x_words[:].bitcast(I32), in_=xt_words[0].bitcast(I32))
+        load_scales(nc.scalar, x_plane, xt_scales)
+        nc.sync.dma_start(out=store_a[1][:], in_=ca_rows[1])
+        load_scales(nc.scalar, w_plane_raw[0], w_scales)
+        nc.sync.dma_start(out=w_raw[0][:].bitcast(I32), in_=words_of[0])
+        nc.sync.dma_start(out=store_a[2][:], in_=ca_rows[2])
+        nc.sync.dma_start(out=w_raw[1][:].bitcast(I32), in_=words_of[1])
+        nc.sync.dma_start(out=store_a[3][:], in_=ca_rows[3])
+        nc.sync.dma_start(list_b[:], offs3)
+        for t in range(PACK):
+            nc.sync.dma_start(out=store_b[t][:], in_=cb_rows[t])
+        nc.sync.dma_start(out=wb_sb[:].bitcast(I32), in_=wb_words[0].bitcast(I32))
+        load_scales(nc.sync, wb_plane, wb_scales)
+
+        def look_up(s, t):
+            store, offsets = ((store_a, list_a), (store_b, list_b))[s]
+            nc.vector.tensor_copy(codes[s][:, t, :], store[t][:].indirect(offsets[:]))
+
+        def deal(s):
+            nc.scalar.copy(
+                out=w_dealt[s][:].rearrange("p (t m) -> p m t", t=PACK),
+                in_=w_raw[s][:].rearrange("p (m t) -> p m t", t=PACK),
+            )
+            nc.vector.tensor_copy(
+                out=w_plane[s][:].rearrange("p (t m) -> p t m", t=PACK),
+                in_=w_plane_raw[s][:].rearrange("p (m t) -> p t m", t=PACK),
+            )
+
+        def first_stage(s):
+            fmt = (E4M3X4, E5M2X4)[s]
+            for t in range(PACK):
+                cols = slice(t * P, (t + 1) * P)
+                acc = psum.tile([P, J], F32, name="acc")
+                nc.tensor.matmul_mx(
+                    out=acc[:], lhsT=w_dealt[s][:, cols].bitcast(fmt), lhsT_scale=w_plane[s][:, cols],
+                    rhs=xg_words[:].bitcast(E2M1X4), rhs_scale=xg_plane[:], start=True, stop=True,
+                )
+                nc.scalar.activation(out=scaled[s][:, t, :], in_=acc[:], func=COPY, scale=steps[s][:, t : t + 1])
+
+        def gate(s, t, cols):
+            nc.vector.tensor_tensor(
+                out=gated[s][:, t, cols], in0=codes[s][:, t, cols].bitcast(FP8), in1=scaled[s][:, t, cols], op=MULT
+            )
+
+        look_up(0, 0)
+        nc.vector.tensor_copy(xg_words[:], x_words[:].indirect(list_x[:]))
+        nc.vector.tensor_copy(xg_plane[:], x_plane[:].indirect(list_x[:]))
+        look_up(0, 1)
+        deal(0)
+        first_stage(0)
+        look_up(0, 2)
+        deal(1)
+        first_stage(1)
+        look_up(0, 3)
+        for t in range(PACK):
+            look_up(1, t)
+        for t in range(PACK):
+            gate(0, t, slice(0, J))
+        halves = [slice(h * HALF, (h + 1) * HALF) for h in range(2)]
+        for cols in halves:
+            for t in range(PACK):
+                gate(1, t, cols)
+
+        hid = [keep.tile([P, HALF * PACK], BF16, name="hid%d" % h, align_bytes=64) for h in range(2)]
+        hid_words = [keep.tile([P, HALF], U32, name="hid_words%d" % h, align_bytes=64) for h in range(2)]
+        hid_plane = [keep.tile([P, HALF], U8, name="hid_plane%d" % h, align_bytes=64) for h in range(2)]
+        for h in range(2):
+            nc.vector.tensor_tensor(
+                out=hid[h][:].rearrange("p (c i t) -> p c t i", i=4, t=PACK),
+                in0=gated[0][:, :, halves[h]].rearrange("p t (c i) -> p c t i", i=4),
+                in1=gated[1][:, :, halves[h]].rearrange("p t (c i) -> p c t i", i=4),
+                op=MAX,
+            )
+        for h in range(2):
+            nc.vector.quantize_mx(out=hid_words[h][:].bitcast(E5M2X4), scales=hid_plane[h][:], in_=hid[h][:])
+        for h in range(2):
+            for u in range(N // P):
+                acc = psum.tile([P, J], F32, name="acc")
+                nc.tensor.matmul_mx(
+                    out=acc[:, 0:HALF], lhsT=wb_sb[:, 2 * u * P : 2 * (u + 1) * P].bitcast(E2M1X4),
+                    lhsT_scale=wb_plane[:, u * P : (u + 1) * P],
+                    rhs=hid_words[h][:].bitcast(E5M2X4), rhs_scale=hid_plane[h][:], start=True, stop=True,
+                )
+                result = keep.tile([P, HALF], F32, name="result%d%d" % (h, u), align_bytes=64)
+                if h == 1 and u == 1:
+                    nc.vector.tensor_copy(out=result[:], in_=acc[:, 0:HALF])
+                    nc.sync.dma_start(out=out[u * P : (u + 1) * P, halves[h]], in_=result[:])
+                else:
+                    nc.scalar.copy(out=result[:], in_=acc[:, 0:HALF])
+                    queue = nc.scalar if h == 1 else nc.sync
+                    queue.dma_start(out=out[u * P : (u + 1) * P, halves[h]], in_=result[:])

@@ -29,6 +29,12 @@ def load_scales(queue, plane, scales):
         queue.dma_start(out=plane[r:P:32, :].bitcast(I32), in_=scales[0, r:16:4, :].bitcast(I32))
 
 
+def load_scale_pairs(queue, staged, scales):
+    rows = scales[0].bitcast(I32).rearrange("(u q r) n -> q r u n", u=2, r=4)
+    for q in range(2):
+        queue.dma_start(out=staged[32 * q : 32 * q + 4, :].bitcast(I32).rearrange("r (u n) -> r u n", u=2), in_=rows[q])
+
+
 def tile_list_twostores_kernel(
     tc, xt_words, xt_scales, w_words, w_scales, w2_words, w2_scales, ca, cb, sa, sb,
     wb_words, wb_scales, offs, offs2, offs3, out,
@@ -46,7 +52,7 @@ def tile_list_twostores_kernel(
         store_a = [keep.tile([P, V], U8, name="store_a%d" % t, align_bytes=64) for t in range(PACK)]
         store_b = [keep.tile([P, D], U8, name="store_b%d" % t, align_bytes=64) for t in range(PACK)]
         w_raw = [keep.tile([P, R], U32, name="w_raw%d" % s, align_bytes=64) for s in range(2)]
-        w_plane_raw = [keep.tile([P, R], U8, name="w_plane_raw%d" % s, align_bytes=64) for s in range(2)]
+        w_plane_raw = [keep.tile([P, 2 * R], U8, name="w_plane_raw%d" % s, align_bytes=64) for s in range(2)]
         w_dealt = [keep.tile([P, R], U32, name="w_dealt%d" % s, align_bytes=64) for s in range(2)]
         w_plane = [keep.tile([P, R], U8, name="w_plane%d" % s, align_bytes=64) for s in range(2)]
         steps = [keep.tile([P, PACK], F32, name="steps%d" % s) for s in range(2)]
@@ -55,7 +61,7 @@ def tile_list_twostores_kernel(
         xg_words = keep.tile([P, J], U16, name="xg_words", align_bytes=64)
         xg_plane = keep.tile([P, J], U8, name="xg_plane", align_bytes=64)
         codes = [keep.tile([P, PACK, J], U8, name="codes%d" % s, align_bytes=64) for s in range(2)]
-        scaled = [keep.tile([P, PACK, J], F32, name="scaled%d" % s, align_bytes=64) for s in range(2)]
+        gates = [keep.tile([P, PACK, J], F32, name="gates%d" % s, align_bytes=64) for s in range(2)]
         gated = [keep.tile([P, PACK, J], F32, name="gated%d" % s, align_bytes=64) for s in range(2)]
 
         ca_rows = ca.rearrange("(p t) v -> t p v", t=PACK)
@@ -65,75 +71,93 @@ def tile_list_twostores_kernel(
         for plane in (x_plane, w_plane_raw[0], w_plane_raw[1], wb_plane):
             nc.vector.memset(plane[:].bitcast(I32), 0)
 
-        nc.gpsimd.dma_start(out=steps[0][:], in_=sa.rearrange("(p t) o -> p (t o)", t=PACK))
-        nc.gpsimd.dma_start(out=steps[1][:], in_=sb.rearrange("(p t) o -> p (t o)", t=PACK))
-        load_scales(nc.gpsimd, w_plane_raw[1], w2_scales)
-
         nc.sync.dma_start(out=store_a[0][:], in_=ca_rows[0])
         nc.sync.dma_start(list_a[:], offs2)
+        nc.sync.dma_start(out=store_a[1][:], in_=ca_rows[1])
         nc.sync.dma_start(list_x[:], offs)
         nc.sync.dma_start(out=x_words[:].bitcast(I32), in_=xt_words[0].bitcast(I32))
-        load_scales(nc.scalar, x_plane, xt_scales)
-        nc.sync.dma_start(out=store_a[1][:], in_=ca_rows[1])
-        load_scales(nc.scalar, w_plane_raw[0], w_scales)
-        nc.sync.dma_start(out=w_raw[0][:].bitcast(I32), in_=words_of[0])
         nc.sync.dma_start(out=store_a[2][:], in_=ca_rows[2])
-        nc.sync.dma_start(out=w_raw[1][:].bitcast(I32), in_=words_of[1])
+        nc.sync.dma_start(out=w_raw[0][:].bitcast(I32), in_=words_of[0])
+        nc.sync.dma_start(out=steps[0][:], in_=sa.rearrange("(p t) o -> p (t o)", t=PACK))
         nc.sync.dma_start(out=store_a[3][:], in_=ca_rows[3])
+        load_scales(nc.sync, x_plane, xt_scales)
+        load_scale_pairs(nc.sync, w_plane_raw[0], w_scales)
         nc.sync.dma_start(list_b[:], offs3)
-        for t in range(PACK):
-            nc.sync.dma_start(out=store_b[t][:], in_=cb_rows[t])
+        nc.sync.dma_start(out=store_b[0][:], in_=cb_rows[0])
+        nc.sync.dma_start(out=steps[1][:], in_=sb.rearrange("(p t) o -> p (t o)", t=PACK))
+        nc.sync.dma_start(out=store_b[1][:], in_=cb_rows[1])
+        nc.sync.dma_start(out=w_raw[1][:].bitcast(I32), in_=words_of[1])
+        load_scale_pairs(nc.sync, w_plane_raw[1], w2_scales)
+        nc.sync.dma_start(out=store_b[2][:], in_=cb_rows[2])
+        nc.sync.dma_start(out=store_b[3][:], in_=cb_rows[3])
         nc.sync.dma_start(out=wb_sb[:].bitcast(I32), in_=wb_words[0].bitcast(I32))
         load_scales(nc.sync, wb_plane, wb_scales)
 
         def look_up(s, t):
             store, offsets = ((store_a, list_a), (store_b, list_b))[s]
             nc.vector.tensor_copy(codes[s][:, t, :], store[t][:].indirect(offsets[:]))
+            nc.scalar.activation(
+                out=gates[s][:, t, :], in_=codes[s][:, t, :].bitcast(FP8), func=COPY, scale=steps[s][:, t : t + 1]
+            )
 
-        def deal(s):
+        def deal_words(s):
             nc.scalar.copy(
                 out=w_dealt[s][:].rearrange("p (t m) -> p m t", t=PACK),
                 in_=w_raw[s][:].rearrange("p (m t) -> p m t", t=PACK),
             )
+
+        def deal_scales(s):
+            nc.vector.tensor_copy(
+                out=w_plane_raw[s][64:P, 0:R].bitcast(I32), in_=w_plane_raw[s][0:64, R : 2 * R].bitcast(I32)
+            )
             nc.vector.tensor_copy(
                 out=w_plane[s][:].rearrange("p (t m) -> p t m", t=PACK),
-                in_=w_plane_raw[s][:].rearrange("p (m t) -> p t m", t=PACK),
+                in_=w_plane_raw[s][:, 0:R].rearrange("p (m t) -> p t m", t=PACK),
             )
+
+        halves = [slice(h * HALF, (h + 1) * HALF) for h in range(2)]
 
         def first_stage(s):
             fmt = (E4M3X4, E5M2X4)[s]
-            for t in range(PACK):
-                cols = slice(t * P, (t + 1) * P)
-                acc = psum.tile([P, J], F32, name="acc")
-                nc.tensor.matmul_mx(
-                    out=acc[:], lhsT=w_dealt[s][:, cols].bitcast(fmt), lhsT_scale=w_plane[s][:, cols],
-                    rhs=xg_words[:].bitcast(E2M1X4), rhs_scale=xg_plane[:], start=True, stop=True,
-                )
-                nc.scalar.activation(out=scaled[s][:, t, :], in_=acc[:], func=COPY, scale=steps[s][:, t : t + 1])
+            banks = []
+            for pair in range(2):
+                acc = psum.tile([P, 2, J], F32, name="acc")
+                for i in range(2):
+                    cols = slice((2 * pair + i) * P, (2 * pair + i + 1) * P)
+                    nc.tensor.matmul_mx(
+                        out=acc[:, i, :], lhsT=w_dealt[s][:, cols].bitcast(fmt), lhsT_scale=w_plane[s][:, cols],
+                        rhs=xg_words[:].bitcast(E2M1X4), rhs_scale=xg_plane[:], start=True, stop=True,
+                    )
+                banks.append(acc)
+            return banks
 
-        def gate(s, t, cols):
+        deal_words(0)
+        look_up(0, 0)
+        look_up(0, 1)
+        nc.vector.tensor_copy(xg_words[:], x_words[:].indirect(list_x[:]))
+        look_up(0, 2)
+        look_up(0, 3)
+        nc.vector.tensor_copy(xg_plane[:], x_plane[:].indirect(list_x[:]))
+        deal_scales(0)
+        sums = [first_stage(0)]
+        look_up(1, 0)
+        look_up(1, 1)
+        deal_words(1)
+        deal_scales(1)
+        sums.append(first_stage(1))
+        look_up(1, 2)
+        look_up(1, 3)
+
+        def gate(s, pair, cols):
+            rows = slice(2 * pair, 2 * pair + 2)
             nc.vector.tensor_tensor(
-                out=gated[s][:, t, cols], in0=codes[s][:, t, cols].bitcast(FP8), in1=scaled[s][:, t, cols], op=MULT
+                out=gated[s][:, rows, cols], in0=sums[s][pair][:, :, cols], in1=gates[s][:, rows, cols], op=MULT
             )
 
-        look_up(0, 0)
-        nc.vector.tensor_copy(xg_words[:], x_words[:].indirect(list_x[:]))
-        nc.vector.tensor_copy(xg_plane[:], x_plane[:].indirect(list_x[:]))
-        look_up(0, 1)
-        deal(0)
-        first_stage(0)
-        look_up(0, 2)
-        deal(1)
-        first_stage(1)
-        look_up(0, 3)
-        for t in range(PACK):
-            look_up(1, t)
-        for t in range(PACK):
-            gate(0, t, slice(0, J))
-        halves = [slice(h * HALF, (h + 1) * HALF) for h in range(2)]
+        for s, pair in ((0, 0), (0, 1), (1, 0)):
+            gate(s, pair, slice(0, J))
         for cols in halves:
-            for t in range(PACK):
-                gate(1, t, cols)
+            gate(1, 1, cols)
 
         hid = [keep.tile([P, HALF * PACK], BF16, name="hid%d" % h, align_bytes=64) for h in range(2)]
         hid_words = [keep.tile([P, HALF], U32, name="hid_words%d" % h, align_bytes=64) for h in range(2)]
@@ -149,17 +173,16 @@ def tile_list_twostores_kernel(
             nc.vector.quantize_mx(out=hid_words[h][:].bitcast(E5M2X4), scales=hid_plane[h][:], in_=hid[h][:])
         for h in range(2):
             for u in range(N // P):
-                acc = psum.tile([P, J], F32, name="acc")
+                acc = psum.tile([P, PACK * HALF], F32, name="acc")
                 nc.tensor.matmul_mx(
                     out=acc[:, 0:HALF], lhsT=wb_sb[:, 2 * u * P : 2 * (u + 1) * P].bitcast(E2M1X4),
                     lhsT_scale=wb_plane[:, u * P : (u + 1) * P],
                     rhs=hid_words[h][:].bitcast(E5M2X4), rhs_scale=hid_plane[h][:], start=True, stop=True,
                 )
                 result = keep.tile([P, HALF], F32, name="result%d%d" % (h, u), align_bytes=64)
-                if h == 1 and u == 1:
+                if u == 1:
                     nc.vector.tensor_copy(out=result[:], in_=acc[:, 0:HALF])
-                    nc.sync.dma_start(out=out[u * P : (u + 1) * P, halves[h]], in_=result[:])
                 else:
                     nc.scalar.copy(out=result[:], in_=acc[:, 0:HALF])
-                    queue = nc.scalar if h == 1 else nc.sync
-                    queue.dma_start(out=out[u * P : (u + 1) * P, halves[h]], in_=result[:])
+                queue = nc.scalar if (h, u) == (1, 0) else nc.sync
+                queue.dma_start(out=out[u * P : (u + 1) * P, halves[h]], in_=result[:])

@@ -73,22 +73,22 @@ def tile_list_twostores_kernel(
 
         nc.sync.dma_start(out=store_a[0][:], in_=ca_rows[0])
         nc.sync.dma_start(list_a[:], offs2)
-        nc.sync.dma_start(out=store_a[1][:], in_=ca_rows[1])
+        nc.sync.dma_start(out=store_a[2][:], in_=ca_rows[2])
         nc.sync.dma_start(list_x[:], offs)
         nc.sync.dma_start(out=x_words[:].bitcast(I32), in_=xt_words[0].bitcast(I32))
-        nc.sync.dma_start(out=store_a[2][:], in_=ca_rows[2])
-        nc.sync.dma_start(out=w_raw[0][:].bitcast(I32), in_=words_of[0])
-        nc.sync.dma_start(out=steps[0][:], in_=sa.rearrange("(p t) o -> p (t o)", t=PACK))
-        nc.sync.dma_start(out=store_a[3][:], in_=ca_rows[3])
-        load_scales(nc.sync, x_plane, xt_scales)
-        load_scale_pairs(nc.sync, w_plane_raw[0], w_scales)
         nc.sync.dma_start(list_b[:], offs3)
         nc.sync.dma_start(out=store_b[0][:], in_=cb_rows[0])
-        nc.sync.dma_start(out=steps[1][:], in_=sb.rearrange("(p t) o -> p (t o)", t=PACK))
-        nc.sync.dma_start(out=store_b[1][:], in_=cb_rows[1])
-        nc.sync.dma_start(out=w_raw[1][:].bitcast(I32), in_=words_of[1])
-        load_scale_pairs(nc.sync, w_plane_raw[1], w2_scales)
+        nc.sync.dma_start(out=w_raw[0][:].bitcast(I32), in_=words_of[0])
+        load_scales(nc.sync, x_plane, xt_scales)
+        load_scale_pairs(nc.sync, w_plane_raw[0], w_scales)
+        nc.sync.dma_start(out=steps[0][:], in_=sa.rearrange("(p t) o -> p (t o)", t=PACK))
         nc.sync.dma_start(out=store_b[2][:], in_=cb_rows[2])
+        load_scale_pairs(nc.sync, w_plane_raw[1], w2_scales)
+        nc.sync.dma_start(out=w_raw[1][:].bitcast(I32), in_=words_of[1])
+        nc.sync.dma_start(out=steps[1][:], in_=sb.rearrange("(p t) o -> p (t o)", t=PACK))
+        nc.sync.dma_start(out=store_a[1][:], in_=ca_rows[1])
+        nc.sync.dma_start(out=store_a[3][:], in_=ca_rows[3])
+        nc.sync.dma_start(out=store_b[1][:], in_=cb_rows[1])
         nc.sync.dma_start(out=store_b[3][:], in_=cb_rows[3])
         nc.sync.dma_start(out=wb_sb[:].bitcast(I32), in_=wb_words[0].bitcast(I32))
         load_scales(nc.sync, wb_plane, wb_scales)
@@ -110,7 +110,7 @@ def tile_list_twostores_kernel(
             nc.vector.tensor_copy(
                 out=w_plane_raw[s][64:P, 0:R].bitcast(I32), in_=w_plane_raw[s][0:64, R : 2 * R].bitcast(I32)
             )
-            nc.vector.tensor_copy(
+            nc.gpsimd.tensor_copy(
                 out=w_plane[s][:].rearrange("p (t m) -> p t m", t=PACK),
                 in_=w_plane_raw[s][:, 0:R].rearrange("p (m t) -> p t m", t=PACK),
             )
@@ -133,20 +133,19 @@ def tile_list_twostores_kernel(
 
         deal_words(0)
         look_up(0, 0)
-        look_up(0, 1)
-        nc.vector.tensor_copy(xg_words[:], x_words[:].indirect(list_x[:]))
         look_up(0, 2)
-        look_up(0, 3)
+        nc.vector.tensor_copy(xg_words[:], x_words[:].indirect(list_x[:]))
+        look_up(1, 0)
         nc.vector.tensor_copy(xg_plane[:], x_plane[:].indirect(list_x[:]))
         deal_scales(0)
         sums = [first_stage(0)]
-        look_up(1, 0)
-        look_up(1, 1)
-        deal_words(1)
-        deal_scales(1)
-        sums.append(first_stage(1))
         look_up(1, 2)
-        look_up(1, 3)
+        deal_scales(1)
+        deal_words(1)
+        sums.append(first_stage(1))
+        for s in range(2):
+            look_up(s, 1)
+            look_up(s, 3)
 
         def gate(s, pair, cols):
             rows = slice(2 * pair, 2 * pair + 2)

from contextlib import ExitStack

import concourse.mybir as mybir

K, T, J, R, V, D, N = 512, 1024, 256, 512, 1024, 1024, 256
FLOPS = 2 * (2 * K * R * J) + 2 * R * N * J

F32 = mybir.dt.float32
BF16 = mybir.dt.bfloat16
I32 = mybir.dt.int32
U32 = mybir.dt.uint32
U16 = mybir.dt.uint16
U8 = mybir.dt.uint8
FP8 = mybir.dt.float8_e4m3fn
E4M3X4 = mybir.dt.float8_e4m3fn_x4
E5M2X4 = mybir.dt.float8_e5m2_x4
E2M1X4 = mybir.dt.float4_e2m1fn_x4
MULT = mybir.AluOpType.mult
MAX = mybir.AluOpType.max
COPY = mybir.ActivationFunctionType.Copy

P = 128
PACK = 4
HALF = J // 2


def load_scales(queue, plane, scales):
    for r in range(4):
        queue.dma_start(out=plane[r:P:32, :].bitcast(I32), in_=scales[0, r:16:4, :].bitcast(I32))


def load_scale_pairs(queue, staged, scales):
    rows = scales[0].bitcast(I32).rearrange("(u q r) n -> q r u n", u=2, r=4)
    for q in range(2):
        queue.dma_start(out=staged[32 * q : 32 * q + 4, :].bitcast(I32).rearrange("r (u n) -> r u n", u=2), in_=rows[q])


def tile_list_twostores_kernel(
    tc, xt_words, xt_scales, w_words, w_scales, w2_words, w2_scales, ca, cb, sa, sb,
    wb_words, wb_scales, offs, offs2, offs3, out,
):
    nc = tc.nc
    with ExitStack() as ctx:
        keep = ctx.enter_context(tc.tile_pool(name="keep", bufs=1))
        psum = ctx.enter_context(tc.psum_pool(name="psum", bufs=8))

        list_x = keep.tile([P, J // 16], U16, name="list_x")
        list_a = keep.tile([P, J // 16], U16, name="list_a")
        list_b = keep.tile([P, J // 16], U16, name="list_b")
        x_words = keep.tile([P, T], U16, name="x_words", align_bytes=64)
        x_plane = keep.tile([P, T], U8, name="x_plane", align_bytes=64)
        store_a = [keep.tile([P, V], U8, name="store_a%d" % t, align_bytes=64) for t in range(PACK)]
        store_b = [keep.tile([P, D], U8, name="store_b%d" % t, align_bytes=64) for t in range(PACK)]
        w_raw = [keep.tile([P, R], U32, name="w_raw%d" % s, align_bytes=64) for s in range(2)]
        w_plane_raw = [keep.tile([P, 2 * R], U8, name="w_plane_raw%d" % s, align_bytes=64) for s in range(2)]
        w_dealt = [keep.tile([P, R], U32, name="w_dealt%d" % s, align_bytes=64) for s in range(2)]
        w_plane = [keep.tile([P, R], U8, name="w_plane%d" % s, align_bytes=64) for s in range(2)]
        steps = [keep.tile([P, PACK], F32, name="steps%d" % s) for s in range(2)]
        wb_sb = keep.tile([P, 2 * N], U8, name="wb_sb", align_bytes=64)
        wb_plane = keep.tile([P, N], U8, name="wb_plane", align_bytes=64)
        xg_words = keep.tile([P, J], U16, name="xg_words", align_bytes=64)
        xg_plane = keep.tile([P, J], U8, name="xg_plane", align_bytes=64)
        codes = [keep.tile([P, PACK, J], U8, name="codes%d" % s, align_bytes=64) for s in range(2)]
        gates = [keep.tile([P, PACK, J], F32, name="gates%d" % s, align_bytes=64) for s in range(2)]
        gated = [keep.tile([P, PACK, J], F32, name="gated%d" % s, align_bytes=64) for s in range(2)]

        ca_rows = ca.rearrange("(p t) v -> t p v", t=PACK)
        cb_rows = cb.rearrange("(p t) v -> t p v", t=PACK)
        words_of = [w.rearrange("a p c r -> p (a c r)").bitcast(I32) for w in (w_words, w2_words)]

        for plane in (x_plane, w_plane_raw[0], w_plane_raw[1], wb_plane):
            nc.vector.memset(plane[:].bitcast(I32), 0)

        nc.sync.dma_start(out=store_a[0][:], in_=ca_rows[0])
        nc.sync.dma_start(list_a[:], offs2)
        nc.sync.dma_start(out=store_a[2][:], in_=ca_rows[2])
        nc.sync.dma_start(list_x[:], offs)
        nc.sync.dma_start(out=x_words[:].bitcast(I32), in_=xt_words[0].bitcast(I32))
        nc.sync.dma_start(list_b[:], offs3)
        nc.sync.dma_start(out=store_b[0][:], in_=cb_rows[0])
        nc.sync.dma_start(out=w_raw[0][:].bitcast(I32), in_=words_of[0])
        load_scales(nc.sync, x_plane, xt_scales)
        load_scale_pairs(nc.sync, w_plane_raw[0], w_scales)
        nc.sync.dma_start(out=steps[0][:], in_=sa.rearrange("(p t) o -> p (t o)", t=PACK))
        nc.sync.dma_start(out=store_b[2][:], in_=cb_rows[2])
        load_scale_pairs(nc.sync, w_plane_raw[1], w2_scales)
        nc.sync.dma_start(out=w_raw[1][:].bitcast(I32), in_=words_of[1])
        nc.sync.dma_start(out=steps[1][:], in_=sb.rearrange("(p t) o -> p (t o)", t=PACK))
        nc.sync.dma_start(out=store_a[1][:], in_=ca_rows[1])
        nc.sync.dma_start(out=store_a[3][:], in_=ca_rows[3])
        nc.sync.dma_start(out=store_b[1][:], in_=cb_rows[1])
        nc.sync.dma_start(out=store_b[3][:], in_=cb_rows[3])
        nc.sync.dma_start(out=wb_sb[:].bitcast(I32), in_=wb_words[0].bitcast(I32))
        load_scales(nc.sync, wb_plane, wb_scales)

        def look_up(s, t):
            store, offsets = ((store_a, list_a), (store_b, list_b))[s]
            nc.vector.tensor_copy(codes[s][:, t, :], store[t][:].indirect(offsets[:]))
            nc.scalar.activation(
                out=gates[s][:, t, :], in_=codes[s][:, t, :].bitcast(FP8), func=COPY, scale=steps[s][:, t : t + 1]
            )

        def deal_words(s):
            nc.scalar.copy(
                out=w_dealt[s][:].rearrange("p (t m) -> p m t", t=PACK),
                in_=w_raw[s][:].rearrange("p (m t) -> p m t", t=PACK),
            )

        def deal_scales(s):
            nc.vector.tensor_copy(
                out=w_plane_raw[s][64:P, 0:R].bitcast(I32), in_=w_plane_raw[s][0:64, R : 2 * R].bitcast(I32)
            )
            nc.gpsimd.tensor_copy(
                out=w_plane[s][:].rearrange("p (t m) -> p t m", t=PACK),
                in_=w_plane_raw[s][:, 0:R].rearrange("p (m t) -> p t m", t=PACK),
            )

        halves = [slice(h * HALF, (h + 1) * HALF) for h in range(2)]

        def first_stage(s):
            fmt = (E4M3X4, E5M2X4)[s]
            banks = []
            for pair in range(2):
                acc = psum.tile([P, 2, J], F32, name="acc")
                for i in range(2):
                    cols = slice((2 * pair + i) * P, (2 * pair + i + 1) * P)
                    nc.tensor.matmul_mx(
                        out=acc[:, i, :], lhsT=w_dealt[s][:, cols].bitcast(fmt), lhsT_scale=w_plane[s][:, cols],
                        rhs=xg_words[:].bitcast(E2M1X4), rhs_scale=xg_plane[:], start=True, stop=True,
                    )
                banks.append(acc)
            return banks

        deal_words(0)
        look_up(0, 0)
        look_up(0, 2)
        nc.vector.tensor_copy(xg_words[:], x_words[:].indirect(list_x[:]))
        look_up(1, 0)
        nc.vector.tensor_copy(xg_plane[:], x_plane[:].indirect(list_x[:]))
        deal_scales(0)
        sums = [first_stage(0)]
        look_up(1, 2)
        deal_scales(1)
        deal_words(1)
        sums.append(first_stage(1))
        for s in range(2):
            look_up(s, 1)
            look_up(s, 3)

        def gate(s, pair, cols):
            rows = slice(2 * pair, 2 * pair + 2)
            nc.vector.tensor_tensor(
                out=gated[s][:, rows, cols], in0=sums[s][pair][:, :, cols], in1=gates[s][:, rows, cols], op=MULT
            )

        for s, pair in ((0, 0), (0, 1), (1, 0)):
            gate(s, pair, slice(0, J))
        for cols in halves:
            gate(1, 1, cols)

        hid = [keep.tile([P, HALF * PACK], BF16, name="hid%d" % h, align_bytes=64) for h in range(2)]
        hid_words = [keep.tile([P, HALF], U32, name="hid_words%d" % h, align_bytes=64) for h in range(2)]
        hid_plane = [keep.tile([P, HALF], U8, name="hid_plane%d" % h, align_bytes=64) for h in range(2)]
        for h in range(2):
            nc.vector.tensor_tensor(
                out=hid[h][:].rearrange("p (c i t) -> p c t i", i=4, t=PACK),
                in0=gated[0][:, :, halves[h]].rearrange("p t (c i) -> p c t i", i=4),
                in1=gated[1][:, :, halves[h]].rearrange("p t (c i) -> p c t i", i=4),
                op=MAX,
            )
        for h in range(2):
            nc.vector.quantize_mx(out=hid_words[h][:].bitcast(E5M2X4), scales=hid_plane[h][:], in_=hid[h][:])
        for h in range(2):
            for u in range(N // P):
                acc = psum.tile([P, PACK * HALF], F32, name="acc")
                nc.tensor.matmul_mx(
                    out=acc[:, 0:HALF], lhsT=wb_sb[:, 2 * u * P : 2 * (u + 1) * P].bitcast(E2M1X4),
                    lhsT_scale=wb_plane[:, u * P : (u + 1) * P],
                    rhs=hid_words[h][:].bitcast(E5M2X4), rhs_scale=hid_plane[h][:], start=True, stop=True,
                )
                result = keep.tile([P, HALF], F32, name="result%d%d" % (h, u), align_bytes=64)
                if u == 1:
                    nc.vector.tensor_copy(out=result[:], in_=acc[:, 0:HALF])
                else:
                    nc.scalar.copy(out=result[:], in_=acc[:, 0:HALF])
                queue = nc.scalar if (h, u) == (1, 0) else nc.sync
                queue.dma_start(out=out[u * P : (u + 1) * P, halves[h]], in_=result[:])
